import numpy as np, ml_dtypes
CORES = [17,81,89,18,82,90]
N = 6
import mx_ref
NC, G = 128, 4
C = np.float32(0.031)
BF = ml_dtypes.bfloat16
def cut(t, i, w=512):
    return t[:, w * i:w * i + w]
def tile(rs):
    return np.stack(rs, axis=2).reshape(128, -1).astype(BF)
def layer(w, X):
    out = []
    for i in range(G):
        for t in range(len(X)):
            p = mx_ref.matmul(mx_ref.quantize(cut(w, len(X) * i + t)), X[t])
            z = p if t == 0 else z + p
        out.append(z)
    return out
def masked(A, E):
    return [(e * (a > 0)) * C for a, e in zip(A, E)]
def setup_inputs(rng):
    def f(*shape):
        return mx_ref.flush((rng.standard_normal(shape, dtype=np.float32) * np.exp2(rng.integers(-2, 3, shape[:-1] + (1,)))).astype(BF))
    return {"x": f(N, 128, 512), "e": f(N, 128, 512), "a": f(N, 128, G * 512), "v": f(N, 128, 4 * NC)}
def setup_inputs_blocks(rng):
    d = setup_inputs(rng)
    for k in ("x", "e", "a", "v"): d[k] = mx_ref.spread(d[k], rng, 4)
    return d
def setup_inputs_wide(rng):
    d = setup_inputs(rng)
    for k in ("x", "e", "a", "v"): d[k] = mx_ref.flush((d[k].astype(np.float32) * np.exp2(rng.integers(-6, 7, (N, 1, 1))).astype(np.float32)).astype(BF))
    return d
def setup_inputs_zeros(rng):
    d = setup_inputs(rng); v = d["x"].reshape(N, 128, -1, 4).copy()
    v[np.broadcast_to((rng.random((N, 1, v.shape[2], 1)) < 0.33), v.shape)] = 0
    d["x"] = v.reshape(d["x"].shape)
    return d
def reference(x, e, a, v):
    T = [mx_ref.quantize(tile(masked(layer(a[j], [mx_ref.quantize(x[j])]), layer(a[j], [mx_ref.quantize(e[j])])))) for j in range(N)]
    y = np.zeros((N, 128, N * NC), np.float32)
    for r in range(N):
        qv = mx_ref.quantize(v[r])
        for j in range(N):
            y[r][:, NC * j:NC * j + NC] = mx_ref.matmul(T[j], qv)
    return {"y": y}

@@ -1,0 +1,190 @@
+from concourse.bass import DstId, RemoteDMATransfer
+from concourse.mybir import dt, AluOpType, ActivationFunctionType
+
+N = 6
+W = 128
+G = 4
+C = 0.031
+
+SCRATCH = {
+    "xe_t": ("sbuf", [128, 1024], "bfloat16"),
+    "a_t": ("sbuf", [128, 2048], "bfloat16"),
+    "v_t": ("sbuf", [128, 512], "bfloat16"),
+    "qxe": ("sbuf", [128, 256], "float8_e4m3fn_x4"),
+    "sxe": ("sbuf", [128, 256], "uint8"),
+    "qa": ("sbuf", [128, 512], "float8_e4m3fn_x4"),
+    "sa": ("sbuf", [128, 512], "uint8"),
+    "qv": ("sbuf", [128, 128], "float8_e4m3fn_x4"),
+    "sv": ("sbuf", [128, 128], "uint8"),
+    "k_t": ("sbuf", [128, 512], "float32"),
+    "h_t": ("sbuf", [128, 512], "bfloat16"),
+    "gq": ("sbuf", [128, N * W], "float8_e4m3fn_x4"),
+    "gs": ("sbuf", [128, N * W], "uint8"),
+    "yo": ("sbuf", [128, N * W], "float32"),
+    "ps": ("psum", [128, 4096], "float32"),
+}
+SEMAPHORES = (["lxe", "lv", "qxe", "qv", "qt", "r", "sent", "st", "cA", "sA", "cB", "sB"]
+              + ["la%d" % i for i in range(G)] + ["qa%d" % i for i in range(G)]
+              + ["u%d" % i for i in range(G)] + ["d%d" % i for i in range(G)] + ["m%d" % i for i in range(G)]
+              + ["c%d" % j for j in range(N)] + ["s%d" % j for j in range(N)]
+              + ["mm%d" % j for j in range(N)] + ["cp%d" % j for j in range(N)])
+
+
+def _bits(mask):
+    return bin(mask).count("1")
+
+
+def _plan(T, topo):
+    cores = list(T.cores)
+    chips = []
+    for c in cores:
+        if topo.chip(c) not in chips:
+            chips.append(topo.chip(c))
+    gate, hub = {}, {}
+    for ch in chips:
+        mem = [c for c in cores if topo.chip(c) == ch]
+        out = [c for c in cores if topo.chip(c) != ch]
+        gate[ch] = [c for c in mem if all(topo.may_write(c, o) for o in out)][0]
+        hub[ch] = [c for c in mem if c != gate[ch]][0]
+    A, B, order = {}, {}, {}
+    for ch in chips:
+        out = [c for c in cores if topo.chip(c) != ch]
+        A[ch] = [c for c in out if topo.may_write(c, hub[ch])]
+        B[ch] = [c for c in out if not topo.may_write(c, hub[ch])]
+        order[ch] = [hub[ch], gate[ch]] + A[ch] + B[ch]
+    return chips, gate, hub, A, B, order
+
+
+def rank_program(g, core, T, topo):
+    rank = T.rank_of(core)
+    if rank is None:
+        return
+    sem = T.sem
+    V, PE, S, SY = g.vector, g.tensor, g.scalar, g.sync
+    chips, gate, hub, A, B, order = _plan(T, topo)
+    me = topo.chip(core)
+    is_hub = hub[me] == core
+    mate_core = gate[me] if is_hub else hub[me]
+    far_hubs = [hub[ch] for ch in chips if ch != me]
+
+    def slot(ch, c):
+        return order[ch].index(c)
+
+    SY.dma_start(T.xe_t[:, 0:512], T.x[:, :]).then_inc(sem.lxe, 16)
+    S.dma_start(T.xe_t[:, 512:1024], T.e[:, :]).then_inc(sem.lxe, 16)
+    for i in range(G):
+        (SY if i % 2 == 0 else S).dma_start(T.a_t[:, 512 * i:512 * i + 512],
+                                            T.a[:, 512 * i:512 * i + 512]).then_inc(sem["la%d" % i], 16)
+    SY.dma_start(T.v_t[:, :], T.v[:, :]).then_inc(sem.lv, 16)
+
+    PE.wait_ge(sem.qxe, 1)
+    for b in range(G):
+        PE.wait_ge(sem["qa%d" % b], 1)
+        for name, bank, col in (("u", b, 0), ("d", G + b, W)):
+            PE.matmul_mx(T.ps[:, 512 * bank:512 * bank + W], T.qa[:, W * b:W * b + W], T.sa[:, W * b:W * b + W],
+                         T.qxe[:, col:col + W], T.sxe[:, col:col + W], True, True).then_inc(sem["%s%d" % (name, b)], 1)
+
+    def quant_a(i):
+        V.wait_ge(sem["la%d" % i], 16)
+        V.quantize_mx(T.qa[:, W * i:W * i + W], T.sa[:, W * i:W * i + W],
+                      T.a_t[:, 512 * i:512 * i + 512]).then_inc(sem["qa%d" % i], 1)
+
+    def result(b):
+        V.wait_ge(sem["u%d" % b], 1)
+        V.tensor_scalar(out=T.k_t[:, W * b:W * b + W], in0=T.ps[:, 512 * b:512 * b + W], scalar1=0.0, scalar2=C,
+                        op0=AluOpType.is_gt, op1=AluOpType.mult).then_inc(sem["m%d" % b], 1)
+        V.wait_ge(sem["m%d" % b], 1)
+        V.wait_ge(sem["d%d" % b], 1)
+        V.tensor_tensor(out=T.h_t[:, b:4 * W:4], in0=T.ps[:, 512 * (G + b):512 * (G + b) + W],
+                        in1=T.k_t[:, W * b:W * b + W], op=AluOpType.mult).then_inc(sem.r, 1)
+
+    V.wait_ge(sem.lxe, 32)
+    V.quantize_mx(T.qxe[:, :], T.sxe[:, :], T.xe_t[:, :]).then_inc(sem.qxe, 1)
+    quant_a(0)
+    for b in range(G):
+        if b + 1 < G:
+            quant_a(b + 1)
+        result(b)
+    own = slot(me, core)
+    V.wait_ge(sem.r, G)
+    V.quantize_mx(T.gq[:, W * own:W * own + W], T.gs[:, W * own:W * own + W], T.h_t[:, :]).then_inc(sem.qt, 1)
+    V.wait_ge(sem.lv, 16)
+    V.quantize_mx(T.qv[:, :], T.sv[:, :], T.v_t[:, :]).then_inc(sem.qv, 1)
+
+    on = topo.mask(core, mate_core)
+    off = topo.mask(core, far_hubs[0])
+    stay = on & ~off
+    sent = [0]
+
+    def view(kind, lo, n):
+        if kind == "c":
+            return T.gq[:, W * lo:W * (lo + n)].bitcast(dt.uint8)
+        return T.gs[:, W * lo:W * (lo + n)]
+
+    def transfer(kind, lo, n, dests, mask, name):
+        ids = []
+        for d, _ in dests:
+            rid, pid, _se = topo.addr(d)
+            ids.append(DstId(rid=rid, pnc=pid))
+        sent[0] += _bits(mask)
+        return RemoteDMATransfer(dst_ids=ids, dma_engine_mask=mask, remote_sem=sem[kind + name],
+                                 srcs=[view(kind, lo, n)], dsts=[view(kind, s, n) for _, s in dests])
+
+    def call(trs):
+        g.remote_dma_fused(trs, local_sem=sem.sent)
+
+    g.wait_ge(sem.qt, 1)
+    if is_hub:
+        for kind in "cs":
+            call([transfer(kind, own, 1, [(mate_core, own)], stay, str(rank))])
+        reach = [h for h in far_hubs if topo.may_write(core, h)]
+        if reach:
+            for kind in "cs":
+                call([transfer(kind, own, 1, [(h, slot(topo.chip(h), core)) for h in reach], off, str(rank))])
+        for run, name in ((A[me], "A"), (B[me], "B")):
+            lo = slot(me, run[0])
+            for kind in "cs":
+                for c in run:
+                    g.wait_ge(sem["%s%d" % (kind, T.rank_of(c))], _bits(off))
+                call([transfer(kind, lo, len(run), [(mate_core, lo)], on, name)])
+    else:
+        for kind in "cs":
+            call([transfer(kind, own, 1, [(mate_core, own)], stay, str(rank)),
+                  transfer(kind, own, 1, [(h, slot(topo.chip(h), core)) for h in far_hubs], off, str(rank))])
+        hr = T.rank_of(mate_core)
+        lo = slot(me, mate_core)
+        blocked = [h for h in far_hubs if not topo.may_write(mate_core, h)]
+        for kind in "cs":
+            g.wait_ge(sem["%s%d" % (kind, hr)], _bits(stay))
+            call([transfer(kind, lo, 1, [(h, slot(topo.chip(h), mate_core)) for h in blocked], off, str(hr))])
+
+    todo = [(core, [])]
+    todo.append((mate_core, [("%s%d" % (k, T.rank_of(mate_core)), _bits(stay)) for k in "cs"]))
+    for run, name in ((A[me], "A"), (B[me], "B")):
+        for c in run:
+            if is_hub:
+                todo.append((c, [("%s%d" % (k, T.rank_of(c)), _bits(off)) for k in "cs"]))
+            else:
+                todo.append((c, [(k + name, _bits(on)) for k in "cs"]))
+    PE.wait_ge(sem.qt, 1)
+    PE.wait_ge(sem.qv, 1)
+    for k, (c, waits) in enumerate(todo):
+        j, lo = T.rank_of(c), slot(me, c)
+        for name, n in waits:
+            PE.wait_ge(sem[name], n)
+        PE.matmul_mx(T.ps[:, 512 * k:512 * k + W], T.gq[:, W * lo:W * lo + W], T.gs[:, W * lo:W * lo + W],
+                     T.qv[:, :], T.sv[:, :], True, True).then_inc(sem["mm%d" % k], 1)
+        dst, src = T.yo[:, W * j:W * j + W], T.ps[:, 512 * k:512 * k + W]
+        if k % 2 == 1:
+            V.wait_ge(sem["mm%d" % k], 1)
+            V.tensor_copy(out=dst, in_=src).then_inc(sem["cp%d" % k], 1)
+            q = SY
+        else:
+            S.wait_ge(sem["mm%d" % k], 1)
+            S.activation(out=dst, in_=src, func=ActivationFunctionType.Copy).then_inc(sem["cp%d" % k], 1)
+            q = S
+        q.wait_ge(sem["cp%d" % k], 1)
+        q.dma_start(T.y[:, W * j:W * j + W], T.yo[:, W * j:W * j + W]).then_inc(sem.st, 16)
+
+    g.wait_ge(sem.sent, sent[0])
+    g.wait_ge(sem.st, 16 * N)

@@ -23,7 +23,7 @@ SCRATCH = {
     "yo": ("sbuf", [128, N * W], "float32"),
     "ps": ("psum", [128, 4096], "float32"),
 }
-SEMAPHORES = (["lxe", "lv", "qxe", "qv", "qt", "r", "sent", "st", "cA", "sA", "cB", "sB"]
+SEMAPHORES = (["lx", "le", "lv", "qx", "qe", "qv", "qt", "r", "sent", "st", "cA", "sA", "cB", "sB"]
               + ["la%d" % i for i in range(G)] + ["qa%d" % i for i in range(G)]
               + ["u%d" % i for i in range(G)] + ["d%d" % i for i in range(G)] + ["m%d" % i for i in range(G)]
               + ["c%d" % j for j in range(N)] + ["s%d" % j for j in range(N)]
@@ -70,41 +70,60 @@ def rank_program(g, core, T, topo):
     def slot(ch, c):
         return order[ch].index(c)
 
-    SY.dma_start(T.xe_t[:, 0:512], T.x[:, :]).then_inc(sem.lxe, 16)
-    S.dma_start(T.xe_t[:, 512:1024], T.e[:, :]).then_inc(sem.lxe, 16)
-    for i in range(G):
-        (SY if i % 2 == 0 else S).dma_start(T.a_t[:, 512 * i:512 * i + 512],
-                                            T.a[:, 512 * i:512 * i + 512]).then_inc(sem["la%d" % i], 16)
+    def load_a(q, i):
+        q.dma_start(T.a_t[:, 512 * i:512 * i + 512], T.a[:, 512 * i:512 * i + 512]).then_inc(sem["la%d" % i], 16)
+
+    SY.dma_start(T.xe_t[:, 0:512], T.x[:, :]).then_inc(sem.lx, 16)
+    load_a(S, 0)
+    SY.dma_start(T.xe_t[:, 512:1024], T.e[:, :]).then_inc(sem.le, 16)
+    load_a(S, 1)
+    load_a(SY, 2)
+    load_a(S, 3)
     SY.dma_start(T.v_t[:, :], T.v[:, :]).then_inc(sem.lv, 16)
 
-    PE.wait_ge(sem.qxe, 1)
     for b in range(G):
         PE.wait_ge(sem["qa%d" % b], 1)
-        for name, bank, col in (("u", b, 0), ("d", G + b, W)):
+        for name, bank, col, need in (("u", b, 0, "qx"), ("d", G + b, W, "qe")):
+            if b == 0:
+                PE.wait_ge(sem[need], 1)
             PE.matmul_mx(T.ps[:, 512 * bank:512 * bank + W], T.qa[:, W * b:W * b + W], T.sa[:, W * b:W * b + W],
                          T.qxe[:, col:col + W], T.sxe[:, col:col + W], True, True).then_inc(sem["%s%d" % (name, b)], 1)
+
+    def quant_xe(half, name):
+        V.wait_ge(sem["l" + name], 16)
+        V.quantize_mx(T.qxe[:, W * half:W * half + W], T.sxe[:, W * half:W * half + W],
+                      T.xe_t[:, 512 * half:512 * half + 512]).then_inc(sem["q" + name], 1)
 
     def quant_a(i):
         V.wait_ge(sem["la%d" % i], 16)
         V.quantize_mx(T.qa[:, W * i:W * i + W], T.sa[:, W * i:W * i + W],
                       T.a_t[:, 512 * i:512 * i + 512]).then_inc(sem["qa%d" % i], 1)
 
-    def result(b):
+    def mask(b):
         V.wait_ge(sem["u%d" % b], 1)
         V.tensor_scalar(out=T.k_t[:, W * b:W * b + W], in0=T.ps[:, 512 * b:512 * b + W], scalar1=0.0, scalar2=C,
                         op0=AluOpType.is_gt, op1=AluOpType.mult).then_inc(sem["m%d" % b], 1)
+
+    def result(b):
         V.wait_ge(sem["m%d" % b], 1)
         V.wait_ge(sem["d%d" % b], 1)
         V.tensor_tensor(out=T.h_t[:, b:4 * W:4], in0=T.ps[:, 512 * (G + b):512 * (G + b) + W],
                         in1=T.k_t[:, W * b:W * b + W], op=AluOpType.mult).then_inc(sem.r, 1)
 
-    V.wait_ge(sem.lxe, 32)
-    V.quantize_mx(T.qxe[:, :], T.sxe[:, :], T.xe_t[:, :]).then_inc(sem.qxe, 1)
+    quant_xe(0, "x")
     quant_a(0)
-    for b in range(G):
-        if b + 1 < G:
-            quant_a(b + 1)
-        result(b)
+    quant_xe(1, "e")
+    quant_a(1)
+    mask(0)
+    quant_a(2)
+    result(0)
+    mask(1)
+    quant_a(3)
+    result(1)
+    mask(2)
+    mask(3)
+    result(2)
+    result(3)
     own = slot(me, core)
     V.wait_ge(sem.r, G)
     V.quantize_mx(T.gq[:, W * own:W * own + W], T.gs[:, W * own:W * own + W], T.h_t[:, :]).then_inc(sem.qt, 1)
@@ -121,13 +140,13 @@ def rank_program(g, core, T, topo):
             return T.gq[:, W * lo:W * (lo + n)].bitcast(dt.uint8)
         return T.gs[:, W * lo:W * (lo + n)]
 
-    def transfer(kind, lo, n, dests, mask, name):
+    def transfer(kind, lo, n, dests, mask_, name):
         ids = []
         for d, _ in dests:
             rid, pid, _se = topo.addr(d)
             ids.append(DstId(rid=rid, pnc=pid))
-        sent[0] += _bits(mask)
-        return RemoteDMATransfer(dst_ids=ids, dma_engine_mask=mask, remote_sem=sem[kind + name],
+        sent[0] += _bits(mask_)
+        return RemoteDMATransfer(dst_ids=ids, dma_engine_mask=mask_, remote_sem=sem[kind + name],
                                  srcs=[view(kind, lo, n)], dsts=[view(kind, s, n) for _, s in dests])
 
     def call(trs):
@@ -149,23 +168,29 @@ def rank_program(g, core, T, topo):
                 call([transfer(kind, lo, len(run), [(mate_core, lo)], on, name)])
     else:
         for kind in "cs":
-            call([transfer(kind, own, 1, [(mate_core, own)], stay, str(rank)),
-                  transfer(kind, own, 1, [(h, slot(topo.chip(h), core)) for h in far_hubs], off, str(rank))])
+            call([transfer(kind, own, 1, [(h, slot(topo.chip(h), core)) for h in far_hubs], off, str(rank))])
         hr = T.rank_of(mate_core)
         lo = slot(me, mate_core)
         blocked = [h for h in far_hubs if not topo.may_write(mate_core, h)]
         for kind in "cs":
             g.wait_ge(sem["%s%d" % (kind, hr)], _bits(stay))
             call([transfer(kind, lo, 1, [(h, slot(topo.chip(h), mate_core)) for h in blocked], off, str(hr))])
+        for kind in "cs":
+            call([transfer(kind, own, 1, [(mate_core, own)], stay, str(rank))])
 
-    todo = [(core, [])]
-    todo.append((mate_core, [("%s%d" % (k, T.rank_of(mate_core)), _bits(stay)) for k in "cs"]))
+    near = (mate_core, [("%s%d" % (k, T.rank_of(mate_core)), _bits(stay)) for k in "cs"])
+    runs = {}
     for run, name in ((A[me], "A"), (B[me], "B")):
+        runs[name] = []
         for c in run:
             if is_hub:
-                todo.append((c, [("%s%d" % (k, T.rank_of(c)), _bits(off)) for k in "cs"]))
+                runs[name].append((c, [("%s%d" % (k, T.rank_of(c)), _bits(off)) for k in "cs"]))
             else:
-                todo.append((c, [(k + name, _bits(on)) for k in "cs"]))
+                runs[name].append((c, [(k + name, _bits(on)) for k in "cs"]))
+    if is_hub:
+        todo = [(core, [])] + runs["A"] + [near] + runs["B"]
+    else:
+        todo = [(core, []), near] + runs["A"] + runs["B"]
     PE.wait_ge(sem.qt, 1)
     PE.wait_ge(sem.qv, 1)
     for k, (c, waits) in enumerate(todo):

from concourse.bass import DstId, RemoteDMATransfer
from concourse.mybir import dt, AluOpType, ActivationFunctionType

N = 6
W = 128
G = 4
C = 0.031

SCRATCH = {
    "xe_t": ("sbuf", [128, 1024], "bfloat16"),
    "a_t": ("sbuf", [128, 2048], "bfloat16"),
    "v_t": ("sbuf", [128, 512], "bfloat16"),
    "qxe": ("sbuf", [128, 256], "float8_e4m3fn_x4"),
    "sxe": ("sbuf", [128, 256], "uint8"),
    "qa": ("sbuf", [128, 512], "float8_e4m3fn_x4"),
    "sa": ("sbuf", [128, 512], "uint8"),
    "qv": ("sbuf", [128, 128], "float8_e4m3fn_x4"),
    "sv": ("sbuf", [128, 128], "uint8"),
    "k_t": ("sbuf", [128, 512], "float32"),
    "h_t": ("sbuf", [128, 512], "bfloat16"),
    "gq": ("sbuf", [128, N * W], "float8_e4m3fn_x4"),
    "gs": ("sbuf", [128, N * W], "uint8"),
    "yo": ("sbuf", [128, N * W], "float32"),
    "ps": ("psum", [128, 4096], "float32"),
}
SEMAPHORES = (["lx", "le", "lv", "qx", "qe", "qv", "qt", "r", "sent", "st", "cA", "sA", "cB", "sB"]
              + ["la%d" % i for i in range(G)] + ["qa%d" % i for i in range(G)]
              + ["u%d" % i for i in range(G)] + ["d%d" % i for i in range(G)] + ["m%d" % i for i in range(G)]
              + ["c%d" % j for j in range(N)] + ["s%d" % j for j in range(N)]
              + ["mm%d" % j for j in range(N)] + ["cp%d" % j for j in range(N)])


def _bits(mask):
    return bin(mask).count("1")


def _plan(T, topo):
    cores = list(T.cores)
    chips = []
    for c in cores:
        if topo.chip(c) not in chips:
            chips.append(topo.chip(c))
    gate, hub = {}, {}
    for ch in chips:
        mem = [c for c in cores if topo.chip(c) == ch]
        out = [c for c in cores if topo.chip(c) != ch]
        gate[ch] = [c for c in mem if all(topo.may_write(c, o) for o in out)][0]
        hub[ch] = [c for c in mem if c != gate[ch]][0]
    A, B, order = {}, {}, {}
    for ch in chips:
        out = [c for c in cores if topo.chip(c) != ch]
        A[ch] = [c for c in out if topo.may_write(c, hub[ch])]
        B[ch] = [c for c in out if not topo.may_write(c, hub[ch])]
        order[ch] = [hub[ch], gate[ch]] + A[ch] + B[ch]
    return chips, gate, hub, A, B, order


def rank_program(g, core, T, topo):
    rank = T.rank_of(core)
    if rank is None:
        return
    sem = T.sem
    V, PE, S, SY = g.vector, g.tensor, g.scalar, g.sync
    chips, gate, hub, A, B, order = _plan(T, topo)
    me = topo.chip(core)
    is_hub = hub[me] == core
    mate_core = gate[me] if is_hub else hub[me]
    far_hubs = [hub[ch] for ch in chips if ch != me]

    def slot(ch, c):
        return order[ch].index(c)

    def load_a(q, i):
        q.dma_start(T.a_t[:, 512 * i:512 * i + 512], T.a[:, 512 * i:512 * i + 512]).then_inc(sem["la%d" % i], 16)

    SY.dma_start(T.xe_t[:, 0:512], T.x[:, :]).then_inc(sem.lx, 16)
    load_a(S, 0)
    SY.dma_start(T.xe_t[:, 512:1024], T.e[:, :]).then_inc(sem.le, 16)
    load_a(S, 1)
    load_a(SY, 2)
    load_a(S, 3)
    SY.dma_start(T.v_t[:, :], T.v[:, :]).then_inc(sem.lv, 16)

    for b in range(G):
        PE.wait_ge(sem["qa%d" % b], 1)
        for name, bank, col, need in (("u", b, 0, "qx"), ("d", G + b, W, "qe")):
            if b == 0:
                PE.wait_ge(sem[need], 1)
            PE.matmul_mx(T.ps[:, 512 * bank:512 * bank + W], T.qa[:, W * b:W * b + W], T.sa[:, W * b:W * b + W],
                         T.qxe[:, col:col + W], T.sxe[:, col:col + W], True, True).then_inc(sem["%s%d" % (name, b)], 1)

    def quant_xe(half, name):
        V.wait_ge(sem["l" + name], 16)
        V.quantize_mx(T.qxe[:, W * half:W * half + W], T.sxe[:, W * half:W * half + W],
                      T.xe_t[:, 512 * half:512 * half + 512]).then_inc(sem["q" + name], 1)

    def quant_a(i):
        V.wait_ge(sem["la%d" % i], 16)
        V.quantize_mx(T.qa[:, W * i:W * i + W], T.sa[:, W * i:W * i + W],
                      T.a_t[:, 512 * i:512 * i + 512]).then_inc(sem["qa%d" % i], 1)

    def mask(b):
        V.wait_ge(sem["u%d" % b], 1)
        V.tensor_scalar(out=T.k_t[:, W * b:W * b + W], in0=T.ps[:, 512 * b:512 * b + W], scalar1=0.0, scalar2=C,
                        op0=AluOpType.is_gt, op1=AluOpType.mult).then_inc(sem["m%d" % b], 1)

    def result(b):
        V.wait_ge(sem["m%d" % b], 1)
        V.wait_ge(sem["d%d" % b], 1)
        V.tensor_tensor(out=T.h_t[:, b:4 * W:4], in0=T.ps[:, 512 * (G + b):512 * (G + b) + W],
                        in1=T.k_t[:, W * b:W * b + W], op=AluOpType.mult).then_inc(sem.r, 1)

    quant_xe(0, "x")
    quant_a(0)
    quant_xe(1, "e")
    quant_a(1)
    mask(0)
    quant_a(2)
    result(0)
    mask(1)
    quant_a(3)
    result(1)
    mask(2)
    mask(3)
    result(2)
    result(3)
    own = slot(me, core)
    V.wait_ge(sem.r, G)
    V.quantize_mx(T.gq[:, W * own:W * own + W], T.gs[:, W * own:W * own + W], T.h_t[:, :]).then_inc(sem.qt, 1)
    V.wait_ge(sem.lv, 16)
    V.quantize_mx(T.qv[:, :], T.sv[:, :], T.v_t[:, :]).then_inc(sem.qv, 1)

    on = topo.mask(core, mate_core)
    off = topo.mask(core, far_hubs[0])
    stay = on & ~off
    sent = [0]

    def view(kind, lo, n):
        if kind == "c":
            return T.gq[:, W * lo:W * (lo + n)].bitcast(dt.uint8)
        return T.gs[:, W * lo:W * (lo + n)]

    def transfer(kind, lo, n, dests, mask_, name):
        ids = []
        for d, _ in dests:
            rid, pid, _se = topo.addr(d)
            ids.append(DstId(rid=rid, pnc=pid))
        sent[0] += _bits(mask_)
        return RemoteDMATransfer(dst_ids=ids, dma_engine_mask=mask_, remote_sem=sem[kind + name],
                                 srcs=[view(kind, lo, n)], dsts=[view(kind, s, n) for _, s in dests])

    def call(trs):
        g.remote_dma_fused(trs, local_sem=sem.sent)

    g.wait_ge(sem.qt, 1)
    if is_hub:
        for kind in "cs":
            call([transfer(kind, own, 1, [(mate_core, own)], stay, str(rank))])
        reach = [h for h in far_hubs if topo.may_write(core, h)]
        if reach:
            for kind in "cs":
                call([transfer(kind, own, 1, [(h, slot(topo.chip(h), core)) for h in reach], off, str(rank))])
        for run, name in ((A[me], "A"), (B[me], "B")):
            lo = slot(me, run[0])
            for kind in "cs":
                for c in run:
                    g.wait_ge(sem["%s%d" % (kind, T.rank_of(c))], _bits(off))
                call([transfer(kind, lo, len(run), [(mate_core, lo)], on, name)])
    else:
        for kind in "cs":
            call([transfer(kind, own, 1, [(h, slot(topo.chip(h), core)) for h in far_hubs], off, str(rank))])
        hr = T.rank_of(mate_core)
        lo = slot(me, mate_core)
        blocked = [h for h in far_hubs if not topo.may_write(mate_core, h)]
        for kind in "cs":
            g.wait_ge(sem["%s%d" % (kind, hr)], _bits(stay))
            call([transfer(kind, lo, 1, [(h, slot(topo.chip(h), mate_core)) for h in blocked], off, str(hr))])
        for kind in "cs":
            call([transfer(kind, own, 1, [(mate_core, own)], stay, str(rank))])

    near = (mate_core, [("%s%d" % (k, T.rank_of(mate_core)), _bits(stay)) for k in "cs"])
    runs = {}
    for run, name in ((A[me], "A"), (B[me], "B")):
        runs[name] = []
        for c in run:
            if is_hub:
                runs[name].append((c, [("%s%d" % (k, T.rank_of(c)), _bits(off)) for k in "cs"]))
            else:
                runs[name].append((c, [(k + name, _bits(on)) for k in "cs"]))
    if is_hub:
        todo = [(core, [])] + runs["A"] + [near] + runs["B"]
    else:
        todo = [(core, []), near] + runs["A"] + runs["B"]
    PE.wait_ge(sem.qt, 1)
    PE.wait_ge(sem.qv, 1)
    for k, (c, waits) in enumerate(todo):
        j, lo = T.rank_of(c), slot(me, c)
        for name, n in waits:
            PE.wait_ge(sem[name], n)
        PE.matmul_mx(T.ps[:, 512 * k:512 * k + W], T.gq[:, W * lo:W * lo + W], T.gs[:, W * lo:W * lo + W],
                     T.qv[:, :], T.sv[:, :], True, True).then_inc(sem["mm%d" % k], 1)
        dst, src = T.yo[:, W * j:W * j + W], T.ps[:, 512 * k:512 * k + W]
        if k % 2 == 1:
            V.wait_ge(sem["mm%d" % k], 1)
            V.tensor_copy(out=dst, in_=src).then_inc(sem["cp%d" % k], 1)
            q = SY
        else:
            S.wait_ge(sem["mm%d" % k], 1)
            S.activation(out=dst, in_=src, func=ActivationFunctionType.Copy).then_inc(sem["cp%d" % k], 1)
            q = S
        q.wait_ge(sem["cp%d" % k], 1)
        q.dma_start(T.y[:, W * j:W * j + W], T.yo[:, W * j:W * j + W]).then_inc(sem.st, 16)

    g.wait_ge(sem.sent, sent[0])
    g.wait_ge(sem.st, 16 * N)
